import numpy as np, ml_dtypes
CORES = [4,20,60,84,92,100,116]
N = 7
KB, QP = 1, 64
ROOT = 5
def setup_inputs(rng):
    q = rng.standard_normal((N, 128, QP), dtype=np.float32) / 4; k = rng.standard_normal((N, 128, KB * 128), dtype=np.float32)
    a = 2 * np.pi * rng.random((N, QP)); s = 400 * rng.random((N, QP)) ** 1.5; q[:, 0, :] = s * np.cos(a); q[:, 1, :] = s * np.sin(a); q[:, 2, :] = 150 * rng.standard_normal((N, QP)); k[:, 2, :] = 1 + k[:, 2, :] / 50
    a = (2 * np.pi * rng.random() + np.pi / 2 * (rng.permutation(N).reshape(N, 1, 1) + 0.5) / N - 0.5 + (np.arange(KB).reshape(1, KB, 1) + rng.random((N, KB, 128))) / KB).reshape(N, KB * 128); k[:, 0, :] = np.cos(a); k[:, 1, :] = np.sin(a)
    for t in range(0, QP, 2):
        j, i = (t // 2) % N, rng.integers(KB * 128); q[ROOT, :2, t] = s[ROOT, t] * k[j, :2, i]; q[ROOT, 3:, t] += k[j, 3:, i] / 8
    return {"q": q.astype(ml_dtypes.bfloat16), "k": k.astype(ml_dtypes.bfloat16), "v": rng.standard_normal((N, 128, KB * 128), dtype=np.float32).astype(ml_dtypes.bfloat16)}
def setup_inputs_big(rng):
    d = setup_inputs(rng)
    for k in ("v",): d[k] = (d[k].astype(np.float32) * 1048576.0).astype(d[k].dtype)
    return d
def setup_inputs_small(rng):
    d = setup_inputs(rng)
    for k in ("v",): d[k] = (d[k].astype(np.float32) * (1 / 1048576.0)).astype(d[k].dtype)
    return d
def reference(q, k, v):
    Q, K, V = q.astype(np.float64), k.astype(np.float64), v.astype(np.float64)
    y = np.full((N, QP, 128), np.nan)
    for r in [ROOT]:
        js = list(range(N))
        S = np.concatenate([K[j].T @ Q[r] for j in js], axis=0)
        P = np.exp(S - S.max(axis=0)); P = P / P.sum(axis=0)
        y[r] = P.T @ np.concatenate([V[j][:, 128 * b:128 * b + 128] for j in js for b in range(KB)], axis=0)
    return {"y": y.astype(ml_dtypes.bfloat16)}

@@ -1,0 +1,156 @@
+from concourse.bass import DstId, RemoteDMATransfer
+from concourse.mybir import AluOpType, AxisListType, ActivationFunctionType
+
+N = 7
+QP = 64
+KP = 128
+BLK = 264
+NE_OFF = 8
+NE_ON = 8
+
+SCRATCH = {
+    "qs": ("sbuf", [128, QP], "bfloat16"),
+    "stg": ("sbuf", [128, 2 * KP], "bfloat16"),
+    "kv": ("sbuf", [128, N * BLK], "bfloat16"),
+    "zer": ("sbuf", [128, 8], "float32"),
+    "one": ("sbuf", [128, 128], "bfloat16"),
+    "eye": ("sbuf", [128, QP], "bfloat16"),
+    "dia": ("sbuf", [128, QP], "bfloat16"),
+    "mc": ("sbuf", [128, 8], "float32"),
+    "nm": ("sbuf", [128, 1], "float32"),
+    "pt": ("sbuf", [128, N * QP], "bfloat16"),
+    "rl": ("sbuf", [128, 1], "float32"),
+    "ys": ("sbuf", [128, 128], "bfloat16"),
+    "po": ("psum", [128, 512], "float32"),
+}
+for _j in range(N):
+    SCRATCH["ps%d" % _j] = ("psum", [128, 512], "float32")
+
+SEMAPHORES = ["ld", "ldq", "sent", "rarr", "cz", "c1", "ci", "co", "mx", "nmd", "dg", "pv", "rc", "yd", "stored"]
+for _j in range(N):
+    SEMAPHORES += ["ka%d" % _j, "va%d" % _j, "st%d" % _j, "sm%d" % _j, "ex%d" % _j]
+
+
+def pick(mask, n, skip=0):
+    bits = [b for b in range(mask.bit_length()) if (mask >> b) & 1]
+    m = 0
+    for b in bits[skip:skip + n]:
+        m |= 1 << b
+    return m
+
+
+def make_plan(T, topo):
+    root = T.cores[T.root]
+    direct = [j for j, c in enumerate(T.cores) if c != root and topo.may_write(c, root)]
+    far = [j for j, c in enumerate(T.cores) if c != root and not topo.may_write(c, root)]
+    busy = [topo.die(T.cores[j]) for j in direct]
+    helpers = {}
+    for j in far:
+        c = T.cores[j]
+        cand = [x for x in range(topo.CORES_PER_CHIP * topo.CHIPS)
+                if topo.chip(x) == topo.chip(c) and x not in T.cores and topo.may_write(x, root)]
+        cand.sort(key=lambda x: (topo.die(x) in busy, x))
+        helpers[j] = (cand[0], cand[1])
+    return root, direct, far, helpers
+
+
+def load_kv(g, T, dst, base, sem):
+    g.sync.dma_start(dst[:, base:base + KP], T.k[:, :]).then_inc(sem, 16)
+    g.scalar.dma_start(dst[:, base + KP:base + 2 * KP], T.v[:, :]).then_inc(sem, 16)
+
+
+def rank_program(g, core, T, topo):
+    root, direct, far, helpers = make_plan(T, topo)
+    rank = T.rank_of(core)
+    rid, pid, se = topo.addr(root)
+
+    for j in far:
+        for piece in range(2):
+            if helpers[j][piece] == core:
+                lo = piece * KP
+                g.wait_ge(T.sem.rarr, NE_ON)
+                g.remote_dma(T.kv[:, j * BLK + lo:j * BLK + lo + KP], T.stg[:, lo:lo + KP],
+                             T.sem[("ka%d", "va%d")[piece] % j], T.sem.sent, pid, rid,
+                             pick(topo.mask(core, root), NE_OFF))
+                g.wait_ge(T.sem.sent, NE_OFF)
+    if rank is None:
+        return
+
+    if rank in direct:
+        load_kv(g, T, T.stg, 0, T.sem.ld)
+        g.wait_ge(T.sem.ld, 32)
+        g.remote_dma(T.kv[:, rank * BLK:rank * BLK + 2 * KP], T.stg[:, :], T.sem["ka%d" % rank], T.sem.sent,
+                     pid, rid, pick(topo.mask(core, root), NE_OFF))
+        g.wait_ge(T.sem.sent, NE_OFF)
+        return
+    if rank in far:
+        load_kv(g, T, T.stg, 0, T.sem.ld)
+        g.wait_ge(T.sem.ld, 32)
+        trs = []
+        for piece in range(2):
+            h = helpers[rank][piece]
+            hr, hp, hs = topo.addr(h)
+            lo = piece * KP
+            trs.append(RemoteDMATransfer(dst_ids=[DstId(rid=hr, pnc=hp)],
+                                         dma_engine_mask=pick(topo.mask(core, h), NE_ON, piece * NE_ON),
+                                         remote_sem=T.sem.rarr, src=T.stg[:, lo:lo + KP], dst=T.stg[:, lo:lo + KP]))
+        g.remote_dma_fused(trs, local_sem=T.sem.sent)
+        g.wait_ge(T.sem.sent, 2 * NE_ON)
+        return
+
+    pe, dve, act = g.tensor, g.vector, g.scalar
+    order = [rank] + direct + far
+    kwait = {rank: ("ka%d" % rank, 32)}
+    vwait = {rank: ("ka%d" % rank, 32)}
+    for j in direct:
+        kwait[j] = vwait[j] = ("ka%d" % j, NE_OFF)
+    for j in far:
+        kwait[j] = ("ka%d" % j, NE_OFF)
+        vwait[j] = ("va%d" % j, NE_OFF)
+    ps = [T["ps%d" % j] for j in range(N)]
+
+    g.sync.dma_start(T.qs[:, :], T.q[:, :]).then_inc(T.sem.ldq, 16)
+    load_kv(g, T, T.kv, rank * BLK, T.sem["ka%d" % rank])
+
+    dve.memset(T.zer[:, :], 0.0).then_inc(T.sem.cz, 1)
+    dve.memset(T.one[:, :], 1.0).then_inc(T.sem.c1, 1)
+    act.wait_ge(T.sem.cz, 1)
+    act.activation(T.kv[:, 2 * KP:N * BLK:BLK], T.zer[:, 0:N], ActivationFunctionType.Exp).then_inc(T.sem.co, 1)
+    g.wait_ge(T.sem.c1, 1)
+    g.affine_select(T.eye[0:QP, :], T.one[0:QP, 0:QP], [[-1, QP]], AluOpType.is_equal, 0.0, 0, 1).then_inc(T.sem.ci, 1)
+
+    pe.wait_ge(T.sem.ldq, 16)
+    for j in order:
+        kj = T.kv[:, j * BLK:j * BLK + KP]
+        pe.wait_ge(T.sem[kwait[j][0]], kwait[j][1])
+        pe.matmul(ps[j][0:QP, QP:QP + KP], T.qs[:, :], kj, True, True).then_inc(T.sem["st%d" % j], 1)
+        pe.matmul(ps[j][:, 0:QP], kj, T.qs[:, :], True, False).then_inc(T.sem["st%d" % j], 1)
+        dve.wait_ge(T.sem["st%d" % j], 2)
+        dve.tensor_reduce(T.mc[0:QP, j:j + 1], ps[j][0:QP, QP:QP + KP], AxisListType.X, AluOpType.max).then_inc(T.sem.mx, 1)
+
+    dve.wait_ge(T.sem.mx, N)
+    dve.tensor_reduce(T.nm[0:QP, :], T.mc[0:QP, 0:N], AxisListType.X, AluOpType.max, negate=True).then_inc(T.sem.nmd, 1)
+    dve.wait_ge(T.sem.nmd, 1)
+    dve.wait_ge(T.sem.ci, 1)
+    dve.tensor_scalar(T.dia[0:QP, :], T.eye[0:QP, :], T.nm[0:QP, :], None, AluOpType.mult).then_inc(T.sem.dg, 1)
+
+    pe.wait_ge(T.sem.dg, 1)
+    for j in order:
+        pe.matmul(ps[j][:, 0:QP], T.one[0:QP, :], T.dia[0:QP, :], False, True).then_inc(T.sem["sm%d" % j], 1)
+        act.wait_ge(T.sem["sm%d" % j], 1)
+        act.activation(T.pt[:, j * QP:(j + 1) * QP], ps[j][:, 0:QP], ActivationFunctionType.Exp).then_inc(T.sem["ex%d" % j], 1)
+
+    pe.wait_ge(T.sem.co, 1)
+    for i, j in enumerate(order):
+        pe.wait_ge(T.sem["ex%d" % j], 1)
+        pe.wait_ge(T.sem[vwait[j][0]], vwait[j][1])
+        pe.matmul(T.po[0:QP, 0:KP + 1], T.pt[:, j * QP:(j + 1) * QP], T.kv[:, j * BLK + KP:j * BLK + 2 * KP + 1],
+                  i == 0, i == N - 1).then_inc(T.sem.pv, 1)
+
+    dve.wait_ge(T.sem.pv, N)
+    dve.reciprocal(T.rl[0:QP, :], T.po[0:QP, KP:KP + 1]).then_inc(T.sem.rc, 1)
+    dve.wait_ge(T.sem.rc, 1)
+    dve.tensor_scalar(T.ys[0:QP, :], T.po[0:QP, 0:KP], T.rl[0:QP, :], None, AluOpType.mult).then_inc(T.sem.yd, 1)
+    g.sync.wait_ge(T.sem.yd, 1)
+    g.sync.dma_start(T.y[:, :], T.ys[0:QP, :]).then_inc(T.sem.stored, 16)
+    g.sync.wait_ge(T.sem.stored, 16)

@@ -7,6 +7,9 @@ KP = 128
 BLK = 264
 NE_OFF = 8
 NE_ON = 8
+D = 20.0
+PRE = 1
+MID = 1
 
 SCRATCH = {
     "qs": ("sbuf", [128, QP], "bfloat16"),
@@ -15,9 +18,11 @@ SCRATCH = {
     "zer": ("sbuf", [128, 8], "float32"),
     "one": ("sbuf", [128, 128], "bfloat16"),
     "eye": ("sbuf", [128, QP], "bfloat16"),
+    "diae": ("sbuf", [128, QP], "bfloat16"),
     "dia": ("sbuf", [128, QP], "bfloat16"),
     "mc": ("sbuf", [128, 8], "float32"),
-    "nm": ("sbuf", [128, 1], "float32"),
+    "nmeb": ("sbuf", [128, 1], "bfloat16"),
+    "nt": ("sbuf", [128, 1], "float32"),
     "pt": ("sbuf", [128, N * QP], "bfloat16"),
     "rl": ("sbuf", [128, 1], "float32"),
     "ys": ("sbuf", [128, 128], "bfloat16"),
@@ -26,15 +31,16 @@ SCRATCH = {
 for _j in range(N):
     SCRATCH["ps%d" % _j] = ("psum", [128, 512], "float32")
 
-SEMAPHORES = ["ld", "ldq", "sent", "rarr", "cz", "c1", "ci", "co", "mx", "nmd", "dg", "pv", "rc", "yd", "stored"]
+SEMAPHORES = ["ldk", "ldv", "ldq", "sent", "rarr", "cz", "c1", "ci", "co", "mx", "med", "nmd", "dge", "dg",
+              "pv", "rc", "yd", "stored"]
 for _j in range(N):
-    SEMAPHORES += ["ka%d" % _j, "va%d" % _j, "st%d" % _j, "sm%d" % _j, "ex%d" % _j]
+    SEMAPHORES += ["ka%d" % _j, "va%d" % _j, "st%d" % _j, "rd%d" % _j, "sm%d" % _j, "ex%d" % _j]
 
 
-def pick(mask, n, skip=0):
+def pick(mask, n):
     bits = [b for b in range(mask.bit_length()) if (mask >> b) & 1]
     m = 0
-    for b in bits[skip:skip + n]:
+    for b in bits[::len(bits) // n][:n]:
         m |= 1 << b
     return m
 
@@ -54,11 +60,6 @@ def make_plan(T, topo):
     return root, direct, far, helpers
 
 
-def load_kv(g, T, dst, base, sem):
-    g.sync.dma_start(dst[:, base:base + KP], T.k[:, :]).then_inc(sem, 16)
-    g.scalar.dma_start(dst[:, base + KP:base + 2 * KP], T.v[:, :]).then_inc(sem, 16)
-
-
 def rank_program(g, core, T, topo):
     root, direct, far, helpers = make_plan(T, topo)
     rank = T.rank_of(core)
@@ -76,76 +77,129 @@ def rank_program(g, core, T, topo):
     if rank is None:
         return
 
-    if rank in direct:
-        load_kv(g, T, T.stg, 0, T.sem.ld)
-        g.wait_ge(T.sem.ld, 32)
-        g.remote_dma(T.kv[:, rank * BLK:rank * BLK + 2 * KP], T.stg[:, :], T.sem["ka%d" % rank], T.sem.sent,
-                     pid, rid, pick(topo.mask(core, root), NE_OFF))
-        g.wait_ge(T.sem.sent, NE_OFF)
-        return
-    if rank in far:
-        load_kv(g, T, T.stg, 0, T.sem.ld)
-        g.wait_ge(T.sem.ld, 32)
-        trs = []
+    if rank != T.root:
+        g.sync.dma_start(T.stg[:, 0:KP], T.k[:, :]).then_inc(T.sem.ldk, 16)
+        g.scalar.dma_start(T.stg[:, KP:2 * KP], T.v[:, :]).then_inc(T.sem.ldv, 16)
+        total = 0
         for piece in range(2):
-            h = helpers[rank][piece]
-            hr, hp, hs = topo.addr(h)
             lo = piece * KP
-            trs.append(RemoteDMATransfer(dst_ids=[DstId(rid=hr, pnc=hp)],
-                                         dma_engine_mask=pick(topo.mask(core, h), NE_ON, piece * NE_ON),
-                                         remote_sem=T.sem.rarr, src=T.stg[:, lo:lo + KP], dst=T.stg[:, lo:lo + KP]))
-        g.remote_dma_fused(trs, local_sem=T.sem.sent)
-        g.wait_ge(T.sem.sent, 2 * NE_ON)
+            g.wait_ge(T.sem[("ldk", "ldv")[piece]], 16)
+            if rank in direct:
+                g.remote_dma(T.kv[:, rank * BLK + lo:rank * BLK + lo + KP], T.stg[:, lo:lo + KP],
+                             T.sem[("ka%d", "va%d")[piece] % rank], T.sem.sent, pid, rid,
+                             pick(topo.mask(core, root), NE_OFF))
+                total += NE_OFF
+            else:
+                h = helpers[rank][piece]
+                hr, hp, hs = topo.addr(h)
+                g.remote_dma(T.stg[:, lo:lo + KP], T.stg[:, lo:lo + KP], T.sem.rarr, T.sem.sent, hp, hr,
+                             pick(topo.mask(core, h), NE_ON))
+                total += NE_ON
+        g.wait_ge(T.sem.sent, total)
         return
 
     pe, dve, act = g.tensor, g.vector, g.scalar
-    order = [rank] + direct + far
-    kwait = {rank: ("ka%d" % rank, 32)}
-    vwait = {rank: ("ka%d" % rank, 32)}
-    for j in direct:
-        kwait[j] = vwait[j] = ("ka%d" % j, NE_OFF)
-    for j in far:
-        kwait[j] = ("ka%d" % j, NE_OFF)
-        vwait[j] = ("va%d" % j, NE_OFF)
+    Exp = ActivationFunctionType.Exp
+    early = [rank] + direct
+    late = list(far)
+    order = early + late
+    col = {j: i for i, j in enumerate(order)}
+    need = {j: NE_OFF for j in order}
+    need[rank] = 16
     ps = [T["ps%d" % j] for j in range(N)]
+    NEa = len(early)
+    NL = len(late)
+
+    def kblk(j):
+        return T.kv[:, j * BLK:j * BLK + KP]
+
+    def vblk(j):
+        return T.kv[:, j * BLK + KP:j * BLK + 2 * KP + 1]
+
+    def ptb(j):
+        return T.pt[:, j * QP:(j + 1) * QP]
 
     g.sync.dma_start(T.qs[:, :], T.q[:, :]).then_inc(T.sem.ldq, 16)
-    load_kv(g, T, T.kv, rank * BLK, T.sem["ka%d" % rank])
+    g.sync.dma_start(kblk(rank), T.k[:, :]).then_inc(T.sem["ka%d" % rank], 16)
+    g.scalar.dma_start(T.kv[:, rank * BLK + KP:rank * BLK + 2 * KP], T.v[:, :]).then_inc(T.sem["va%d" % rank], 16)
 
     dve.memset(T.zer[:, :], 0.0).then_inc(T.sem.cz, 1)
     dve.memset(T.one[:, :], 1.0).then_inc(T.sem.c1, 1)
     act.wait_ge(T.sem.cz, 1)
-    act.activation(T.kv[:, 2 * KP:N * BLK:BLK], T.zer[:, 0:N], ActivationFunctionType.Exp).then_inc(T.sem.co, 1)
+    act.activation(T.kv[:, 2 * KP:N * BLK:BLK], T.zer[:, 0:N], Exp).then_inc(T.sem.co, 1)
     g.wait_ge(T.sem.c1, 1)
     g.affine_select(T.eye[0:QP, :], T.one[0:QP, 0:QP], [[-1, QP]], AluOpType.is_equal, 0.0, 0, 1).then_inc(T.sem.ci, 1)
 
+    spare = [ps[j] for j in late] + [T.po]
+    where = {rank: ps[rank][0:QP, QP:QP + KP]}
+    for i, j in enumerate(direct):
+        where[j] = spare[i % len(spare)][0:QP, KP:2 * KP]
     pe.wait_ge(T.sem.ldq, 16)
-    for j in order:
-        kj = T.kv[:, j * BLK:j * BLK + KP]
-        pe.wait_ge(T.sem[kwait[j][0]], kwait[j][1])
-        pe.matmul(ps[j][0:QP, QP:QP + KP], T.qs[:, :], kj, True, True).then_inc(T.sem["st%d" % j], 1)
-        pe.matmul(ps[j][:, 0:QP], kj, T.qs[:, :], True, False).then_inc(T.sem["st%d" % j], 1)
-        dve.wait_ge(T.sem["st%d" % j], 2)
-        dve.tensor_reduce(T.mc[0:QP, j:j + 1], ps[j][0:QP, QP:QP + KP], AxisListType.X, AluOpType.max).then_inc(T.sem.mx, 1)
-
-    dve.wait_ge(T.sem.mx, N)
-    dve.tensor_reduce(T.nm[0:QP, :], T.mc[0:QP, 0:N], AxisListType.X, AluOpType.max, negate=True).then_inc(T.sem.nmd, 1)
-    dve.wait_ge(T.sem.nmd, 1)
+    pe.wait_ge(T.sem["ka%d" % rank], need[rank])
+    pe.matmul(where[rank], T.qs[:, :], kblk(rank), True, True).then_inc(T.sem["st%d" % rank], 1)
+    pe.matmul(ps[rank][:, 0:QP], kblk(rank), T.qs[:, :], True, False).then_inc(T.sem["st%d" % rank], 1)
+    for i, j in enumerate(direct):
+        pe.wait_ge(T.sem["ka%d" % j], need[j])
+        if i >= len(spare):
+            pe.wait_ge(T.sem["rd%d" % direct[i - len(spare)]], 1)
+        pe.matmul(where[j], T.qs[:, :], kblk(j), True, True).then_inc(T.sem["st%d" % j], 1)
+    for j in direct:
+        pe.matmul(ps[j][:, 0:QP], kblk(j), T.qs[:, :], True, False)
+    for j in early:
+        dve.wait_ge(T.sem["st%d" % j], 2 if j == rank else 1)
+        dve.tensor_reduce(T.mc[0:QP, col[j]:col[j] + 1], where[j], AxisListType.X,
+                          AluOpType.max).then_inc(T.sem["rd%d" % j], 1)
+    for j in early:
+        dve.wait_ge(T.sem["rd%d" % j], 1)
+    dve.tensor_reduce(T.nmeb[0:QP, :], T.mc[0:QP, 0:NEa], AxisListType.X, AluOpType.max,
+                      negate=True).then_inc(T.sem.med, 1)
+    dve.wait_ge(T.sem.med, 1)
     dve.wait_ge(T.sem.ci, 1)
-    dve.tensor_scalar(T.dia[0:QP, :], T.eye[0:QP, :], T.nm[0:QP, :], None, AluOpType.mult).then_inc(T.sem.dg, 1)
-
-    pe.wait_ge(T.sem.dg, 1)
-    for j in order:
-        pe.matmul(ps[j][:, 0:QP], T.one[0:QP, :], T.dia[0:QP, :], False, True).then_inc(T.sem["sm%d" % j], 1)
+    dve.tensor_scalar(T.diae[0:QP, :], T.eye[0:QP, :], T.nmeb[0:QP, :], None, AluOpType.mult).then_inc(T.sem.dge, 1)
+    dve.tensor_scalar(T.mc[0:QP, NEa:NEa + 1], T.nmeb[0:QP, :], -1.0, D, AluOpType.mult,
+                      AluOpType.add).then_inc(T.sem.mx, 1)
+    pe.wait_ge(T.sem.dge, 1)
+    for j in early:
+        pe.matmul(ps[j][:, 0:QP], T.one[0:QP, :], T.diae[0:QP, :], False, True).then_inc(T.sem["sm%d" % j], 1)
         act.wait_ge(T.sem["sm%d" % j], 1)
-        act.activation(T.pt[:, j * QP:(j + 1) * QP], ps[j][:, 0:QP], ActivationFunctionType.Exp).then_inc(T.sem["ex%d" % j], 1)
+        act.activation(ptb(j), ps[j][:, 0:QP], Exp).then_inc(T.sem["ex%d" % j], 1)
+
+    def product(j):
+        i = col[j]
+        pe.wait_ge(T.sem["ex%d" % j], 1)
+        pe.wait_ge(T.sem["va%d" % j], need[j])
+        pe.matmul(T.po[0:QP, 0:KP + 1], ptb(j), vblk(j), i == 0, i == N - 1).then_inc(T.sem.pv, 1)
 
     pe.wait_ge(T.sem.co, 1)
-    for i, j in enumerate(order):
-        pe.wait_ge(T.sem["ex%d" % j], 1)
-        pe.wait_ge(T.sem[vwait[j][0]], vwait[j][1])
-        pe.matmul(T.po[0:QP, 0:KP + 1], T.pt[:, j * QP:(j + 1) * QP], T.kv[:, j * BLK + KP:j * BLK + 2 * KP + 1],
-                  i == 0, i == N - 1).then_inc(T.sem.pv, 1)
+    for j in order[0:PRE]:
+        product(j)
+
+    for i, j in enumerate(late):
+        pe.wait_ge(T.sem["ex%d" % early[i]], 1)
+        pe.wait_ge(T.sem["ka%d" % j], need[j])
+        pe.matmul(ps[early[i]][0:QP, 0:KP], T.qs[:, :], kblk(j), True, True).then_inc(T.sem["st%d" % j], 1)
+        dve.wait_ge(T.sem["st%d" % j], 1)
+        dve.tensor_reduce(T.mc[0:QP, NEa + 1 + i:NEa + 2 + i], ps[early[i]][0:QP, 0:KP], AxisListType.X,
+                          AluOpType.max).then_inc(T.sem.mx, 1)
+    for j in late:
+        pe.matmul(ps[j][:, 0:QP], kblk(j), T.qs[:, :], True, False)
+    for j in order[PRE:PRE + MID]:
+        product(j)
+
+    dve.wait_ge(T.sem.mx, NL + 1)
+    dve.tensor_reduce(T.nt[0:QP, :], T.mc[0:QP, NEa:NEa + 1 + NL], AxisListType.X, AluOpType.max,
+                      negate=True).then_inc(T.sem.nmd, 1)
+    dve.wait_ge(T.sem.nmd, 1)
+    dve.tensor_scalar(T.dia[0:QP, :], T.eye[0:QP, :], T.nt[0:QP, :], D, AluOpType.mult, AluOpType.add).then_inc(T.sem.dg, 1)
+
+    pe.wait_ge(T.sem.dg, 1)
+    for j in late:
+        pe.matmul(ps[j][:, 0:QP], T.one[0:QP, :], T.dia[0:QP, :], False, True).then_inc(T.sem["sm%d" % j], 1)
+        act.wait_ge(T.sem["sm%d" % j], 1)
+        act.activation(ptb(j), ps[j][:, 0:QP], Exp, bias=-(QP - 1) * D).then_inc(T.sem["ex%d" % j], 1)
+
+    for j in order[PRE + MID:]:
+        product(j)
 
     dve.wait_ge(T.sem.pv, N)
     dve.reciprocal(T.rl[0:QP, :], T.po[0:QP, KP:KP + 1]).then_inc(T.sem.rc, 1)

from concourse.bass import DstId, RemoteDMATransfer
from concourse.mybir import AluOpType, AxisListType, ActivationFunctionType

N = 7
QP = 64
KP = 128
BLK = 264
NE_OFF = 8
NE_ON = 8
D = 20.0
PRE = 1
MID = 1

SCRATCH = {
    "qs": ("sbuf", [128, QP], "bfloat16"),
    "stg": ("sbuf", [128, 2 * KP], "bfloat16"),
    "kv": ("sbuf", [128, N * BLK], "bfloat16"),
    "zer": ("sbuf", [128, 8], "float32"),
    "one": ("sbuf", [128, 128], "bfloat16"),
    "eye": ("sbuf", [128, QP], "bfloat16"),
    "diae": ("sbuf", [128, QP], "bfloat16"),
    "dia": ("sbuf", [128, QP], "bfloat16"),
    "mc": ("sbuf", [128, 8], "float32"),
    "nmeb": ("sbuf", [128, 1], "bfloat16"),
    "nt": ("sbuf", [128, 1], "float32"),
    "pt": ("sbuf", [128, N * QP], "bfloat16"),
    "rl": ("sbuf", [128, 1], "float32"),
    "ys": ("sbuf", [128, 128], "bfloat16"),
    "po": ("psum", [128, 512], "float32"),
}
for _j in range(N):
    SCRATCH["ps%d" % _j] = ("psum", [128, 512], "float32")

SEMAPHORES = ["ldk", "ldv", "ldq", "sent", "rarr", "cz", "c1", "ci", "co", "mx", "med", "nmd", "dge", "dg",
              "pv", "rc", "yd", "stored"]
for _j in range(N):
    SEMAPHORES += ["ka%d" % _j, "va%d" % _j, "st%d" % _j, "rd%d" % _j, "sm%d" % _j, "ex%d" % _j]


def pick(mask, n):
    bits = [b for b in range(mask.bit_length()) if (mask >> b) & 1]
    m = 0
    for b in bits[::len(bits) // n][:n]:
        m |= 1 << b
    return m


def make_plan(T, topo):
    root = T.cores[T.root]
    direct = [j for j, c in enumerate(T.cores) if c != root and topo.may_write(c, root)]
    far = [j for j, c in enumerate(T.cores) if c != root and not topo.may_write(c, root)]
    busy = [topo.die(T.cores[j]) for j in direct]
    helpers = {}
    for j in far:
        c = T.cores[j]
        cand = [x for x in range(topo.CORES_PER_CHIP * topo.CHIPS)
                if topo.chip(x) == topo.chip(c) and x not in T.cores and topo.may_write(x, root)]
        cand.sort(key=lambda x: (topo.die(x) in busy, x))
        helpers[j] = (cand[0], cand[1])
    return root, direct, far, helpers


def rank_program(g, core, T, topo):
    root, direct, far, helpers = make_plan(T, topo)
    rank = T.rank_of(core)
    rid, pid, se = topo.addr(root)

    for j in far:
        for piece in range(2):
            if helpers[j][piece] == core:
                lo = piece * KP
                g.wait_ge(T.sem.rarr, NE_ON)
                g.remote_dma(T.kv[:, j * BLK + lo:j * BLK + lo + KP], T.stg[:, lo:lo + KP],
                             T.sem[("ka%d", "va%d")[piece] % j], T.sem.sent, pid, rid,
                             pick(topo.mask(core, root), NE_OFF))
                g.wait_ge(T.sem.sent, NE_OFF)
    if rank is None:
        return

    if rank != T.root:
        g.sync.dma_start(T.stg[:, 0:KP], T.k[:, :]).then_inc(T.sem.ldk, 16)
        g.scalar.dma_start(T.stg[:, KP:2 * KP], T.v[:, :]).then_inc(T.sem.ldv, 16)
        total = 0
        for piece in range(2):
            lo = piece * KP
            g.wait_ge(T.sem[("ldk", "ldv")[piece]], 16)
            if rank in direct:
                g.remote_dma(T.kv[:, rank * BLK + lo:rank * BLK + lo + KP], T.stg[:, lo:lo + KP],
                             T.sem[("ka%d", "va%d")[piece] % rank], T.sem.sent, pid, rid,
                             pick(topo.mask(core, root), NE_OFF))
                total += NE_OFF
            else:
                h = helpers[rank][piece]
                hr, hp, hs = topo.addr(h)
                g.remote_dma(T.stg[:, lo:lo + KP], T.stg[:, lo:lo + KP], T.sem.rarr, T.sem.sent, hp, hr,
                             pick(topo.mask(core, h), NE_ON))
                total += NE_ON
        g.wait_ge(T.sem.sent, total)
        return

    pe, dve, act = g.tensor, g.vector, g.scalar
    Exp = ActivationFunctionType.Exp
    early = [rank] + direct
    late = list(far)
    order = early + late
    col = {j: i for i, j in enumerate(order)}
    need = {j: NE_OFF for j in order}
    need[rank] = 16
    ps = [T["ps%d" % j] for j in range(N)]
    NEa = len(early)
    NL = len(late)

    def kblk(j):
        return T.kv[:, j * BLK:j * BLK + KP]

    def vblk(j):
        return T.kv[:, j * BLK + KP:j * BLK + 2 * KP + 1]

    def ptb(j):
        return T.pt[:, j * QP:(j + 1) * QP]

    g.sync.dma_start(T.qs[:, :], T.q[:, :]).then_inc(T.sem.ldq, 16)
    g.sync.dma_start(kblk(rank), T.k[:, :]).then_inc(T.sem["ka%d" % rank], 16)
    g.scalar.dma_start(T.kv[:, rank * BLK + KP:rank * BLK + 2 * KP], T.v[:, :]).then_inc(T.sem["va%d" % rank], 16)

    dve.memset(T.zer[:, :], 0.0).then_inc(T.sem.cz, 1)
    dve.memset(T.one[:, :], 1.0).then_inc(T.sem.c1, 1)
    act.wait_ge(T.sem.cz, 1)
    act.activation(T.kv[:, 2 * KP:N * BLK:BLK], T.zer[:, 0:N], Exp).then_inc(T.sem.co, 1)
    g.wait_ge(T.sem.c1, 1)
    g.affine_select(T.eye[0:QP, :], T.one[0:QP, 0:QP], [[-1, QP]], AluOpType.is_equal, 0.0, 0, 1).then_inc(T.sem.ci, 1)

    spare = [ps[j] for j in late] + [T.po]
    where = {rank: ps[rank][0:QP, QP:QP + KP]}
    for i, j in enumerate(direct):
        where[j] = spare[i % len(spare)][0:QP, KP:2 * KP]
    pe.wait_ge(T.sem.ldq, 16)
    pe.wait_ge(T.sem["ka%d" % rank], need[rank])
    pe.matmul(where[rank], T.qs[:, :], kblk(rank), True, True).then_inc(T.sem["st%d" % rank], 1)
    pe.matmul(ps[rank][:, 0:QP], kblk(rank), T.qs[:, :], True, False).then_inc(T.sem["st%d" % rank], 1)
    for i, j in enumerate(direct):
        pe.wait_ge(T.sem["ka%d" % j], need[j])
        if i >= len(spare):
            pe.wait_ge(T.sem["rd%d" % direct[i - len(spare)]], 1)
        pe.matmul(where[j], T.qs[:, :], kblk(j), True, True).then_inc(T.sem["st%d" % j], 1)
    for j in direct:
        pe.matmul(ps[j][:, 0:QP], kblk(j), T.qs[:, :], True, False)
    for j in early:
        dve.wait_ge(T.sem["st%d" % j], 2 if j == rank else 1)
        dve.tensor_reduce(T.mc[0:QP, col[j]:col[j] + 1], where[j], AxisListType.X,
                          AluOpType.max).then_inc(T.sem["rd%d" % j], 1)
    for j in early:
        dve.wait_ge(T.sem["rd%d" % j], 1)
    dve.tensor_reduce(T.nmeb[0:QP, :], T.mc[0:QP, 0:NEa], AxisListType.X, AluOpType.max,
                      negate=True).then_inc(T.sem.med, 1)
    dve.wait_ge(T.sem.med, 1)
    dve.wait_ge(T.sem.ci, 1)
    dve.tensor_scalar(T.diae[0:QP, :], T.eye[0:QP, :], T.nmeb[0:QP, :], None, AluOpType.mult).then_inc(T.sem.dge, 1)
    dve.tensor_scalar(T.mc[0:QP, NEa:NEa + 1], T.nmeb[0:QP, :], -1.0, D, AluOpType.mult,
                      AluOpType.add).then_inc(T.sem.mx, 1)
    pe.wait_ge(T.sem.dge, 1)
    for j in early:
        pe.matmul(ps[j][:, 0:QP], T.one[0:QP, :], T.diae[0:QP, :], False, True).then_inc(T.sem["sm%d" % j], 1)
        act.wait_ge(T.sem["sm%d" % j], 1)
        act.activation(ptb(j), ps[j][:, 0:QP], Exp).then_inc(T.sem["ex%d" % j], 1)

    def product(j):
        i = col[j]
        pe.wait_ge(T.sem["ex%d" % j], 1)
        pe.wait_ge(T.sem["va%d" % j], need[j])
        pe.matmul(T.po[0:QP, 0:KP + 1], ptb(j), vblk(j), i == 0, i == N - 1).then_inc(T.sem.pv, 1)

    pe.wait_ge(T.sem.co, 1)
    for j in order[0:PRE]:
        product(j)

    for i, j in enumerate(late):
        pe.wait_ge(T.sem["ex%d" % early[i]], 1)
        pe.wait_ge(T.sem["ka%d" % j], need[j])
        pe.matmul(ps[early[i]][0:QP, 0:KP], T.qs[:, :], kblk(j), True, True).then_inc(T.sem["st%d" % j], 1)
        dve.wait_ge(T.sem["st%d" % j], 1)
        dve.tensor_reduce(T.mc[0:QP, NEa + 1 + i:NEa + 2 + i], ps[early[i]][0:QP, 0:KP], AxisListType.X,
                          AluOpType.max).then_inc(T.sem.mx, 1)
    for j in late:
        pe.matmul(ps[j][:, 0:QP], kblk(j), T.qs[:, :], True, False)
    for j in order[PRE:PRE + MID]:
        product(j)

    dve.wait_ge(T.sem.mx, NL + 1)
    dve.tensor_reduce(T.nt[0:QP, :], T.mc[0:QP, NEa:NEa + 1 + NL], AxisListType.X, AluOpType.max,
                      negate=True).then_inc(T.sem.nmd, 1)
    dve.wait_ge(T.sem.nmd, 1)
    dve.tensor_scalar(T.dia[0:QP, :], T.eye[0:QP, :], T.nt[0:QP, :], D, AluOpType.mult, AluOpType.add).then_inc(T.sem.dg, 1)

    pe.wait_ge(T.sem.dg, 1)
    for j in late:
        pe.matmul(ps[j][:, 0:QP], T.one[0:QP, :], T.dia[0:QP, :], False, True).then_inc(T.sem["sm%d" % j], 1)
        act.wait_ge(T.sem["sm%d" % j], 1)
        act.activation(ptb(j), ps[j][:, 0:QP], Exp, bias=-(QP - 1) * D).then_inc(T.sem["ex%d" % j], 1)

    for j in order[PRE + MID:]:
        product(j)

    dve.wait_ge(T.sem.pv, N)
    dve.reciprocal(T.rl[0:QP, :], T.po[0:QP, KP:KP + 1]).then_inc(T.sem.rc, 1)
    dve.wait_ge(T.sem.rc, 1)
    dve.tensor_scalar(T.ys[0:QP, :], T.po[0:QP, 0:KP], T.rl[0:QP, :], None, AluOpType.mult).then_inc(T.sem.yd, 1)
    g.sync.wait_ge(T.sem.yd, 1)
    g.sync.dma_start(T.y[:, :], T.ys[0:QP, :]).then_inc(T.sem.stored, 16)
    g.sync.wait_ge(T.sem.stored, 16)
